import numpy as np
import ml_dtypes


def mxq(x, axis, fmt="e4m3"):
    dtype, down = {"e4m3": (ml_dtypes.float8_e4m3fn, 7), "e5m2": (ml_dtypes.float8_e5m2, 14)}[fmt]
    v = np.moveaxis(np.asarray(x, np.float32).astype(ml_dtypes.bfloat16).astype(np.float64), axis, -1)
    blocks = v.reshape(v.shape[:-1] + (-1, 32))
    amax = np.abs(blocks).max(-1, keepdims=True)
    byte = np.maximum(np.where(amax > 0, np.frexp(amax)[1] - 1 + 127, 0) - down, 1)
    scale = np.exp2(byte - 127.0)
    codes = (blocks / scale).astype(np.float32).astype(dtype).astype(np.float64)
    return np.moveaxis((codes * scale).reshape(v.shape), -1, axis)


WIDE = False


def mx_kscale(k):
    if not WIDE:
        return np.ones(k)
    levels = np.array([10, -10, 5, -5, 0])
    if k % 512:
        return np.exp2(np.random.permutation(np.resize(levels, k // 32))).repeat(32)
    a = np.empty((k // 512, 16))
    for p in range(k // 512):
        a[p, :8] = np.random.permutation(np.resize(levels, 8))
        for g in range(8):
            far = levels[np.abs(levels - a[p, g]) >= 10]
            a[p, g + 8] = far[np.random.randint(len(far))]
    return np.exp2(a.ravel()).repeat(32)


def f64(x):
    return np.asarray(x).astype(np.float64)


def striped(idx):
    return np.tile(np.asarray(idx).reshape(-1, 16).T, (8, 1)).astype(np.uint16)


def unstriped(offs):
    return offs[:16].T.reshape(-1).astype(np.int64)

def sigmoid(v):
    return 1.0 / (1.0 + np.exp(-v))


def bf(x):
    return np.asarray(x, np.float32).astype(ml_dtypes.bfloat16)


def planes(Y):
    r, m = Y.shape
    b = f64(bf(Y)).reshape(r // 32, 32, m)
    amax = np.abs(b).max(1)
    byte = np.clip(np.where(amax > 0, np.frexp(amax)[1] - 1 + 127 - 7, 1), 1, 254)
    codes = (b * np.exp2(127.0 - byte)[:, None, :]).reshape(r, m).astype(np.float32).astype(ml_dtypes.float8_e4m3fn).view(np.uint8)
    words = codes.reshape(r // 512, 128, 4, m).transpose(0, 1, 3, 2)
    return np.ascontiguousarray(words), np.ascontiguousarray(byte.astype(np.uint8).reshape(r // 512, 16, m))


B, N, T, D, NQ = 1, 512, 2048, 512, 256


def setup_inputs():
    n = np.random.standard_normal
    idx = np.random.permutation(T)[:B * N]
    idx2 = np.random.permutation(1024)[:B * N]
    s = mx_kscale(D)[:, None]
    return {
        "qT": (n((B, D, NQ)) * s * (1.00 / np.sqrt(D))).astype(np.float32),
        "kT": (np.clip(np.round(n((D, T)) * 16), -64, 64) / 16 / s).astype(np.float32),
        "gT": (np.random.randint(0, 65, (D, 1024)) / 64.0).astype(np.float32),
        "th": (n((B, 1, NQ)) + 1).astype(np.float32),
        "offs": striped(idx),
        "offs2": striped(idx2),
    }


def reference(qT, kT, gT, th, offs, offs2):
    idx = unstriped(offs)
    idx2 = unstriped(offs2)
    pick = lambda x, which: x[:, which].reshape(x.shape[0], B, -1).transpose(1, 0, 2)
    kg = pick(f64(kT), idx)
    gg = pick(f64(gT), idx2)
    ug = mxq(kg * gg, 1, "e4m3")
    qq = mxq(f64(qT), 1, "e4m3")
    a = ug.transpose(0, 2, 1) @ qq
    y = sigmoid(a - f64(th))
    Y = y[0]
    words, scales = planes(Y)
    return Y, words, scales

@@ -1,0 +1,149 @@
+from contextlib import ExitStack
+
+import concourse.mybir as mybir
+from concourse.masks import make_identity
+
+F32 = mybir.dt.float32
+BF16 = mybir.dt.bfloat16
+I32 = mybir.dt.int32
+U16 = mybir.dt.uint16
+U8 = mybir.dt.uint8
+FP8X4 = mybir.dt.float8_e4m3fn_x4
+MULT = mybir.AluOpType.mult
+SUBTRACT = mybir.AluOpType.subtract
+SIGMOID = mybir.ActivationFunctionType.Sigmoid
+
+P = 128
+PACK = 4
+SLOTS, TOKENS, GATES, D, NQ = 512, 2048, 1024, 512, 256
+HALVES = 2
+QH = NQ // HALVES
+FLOPS = 2 * SLOTS * D * NQ
+
+
+def tile_attend_plw_gatekey_f_topk_kernel(tc, qT, kT, gT, th, offs, offs2, out_0, out_1, out_2):
+    nc = tc.nc
+    with ExitStack() as ctx:
+        held = ctx.enter_context(tc.tile_pool(name="held", bufs=1))
+        psum = ctx.enter_context(tc.psum_pool(name="psum", bufs=1))
+
+        key_list = held.tile([P, SLOTS // 16], U16, name="key_list")
+        gate_list = held.tile([P, SLOTS // 16], U16, name="gate_list")
+        th_cols = held.tile([P, 2], F32, name="th_cols")
+        gates = [held.tile([P, GATES], F32, name="gates%d" % t) for t in range(PACK)]
+        keys = [held.tile([P, TOKENS], F32, name="keys%d" % t) for t in range(PACK)]
+        q_raw = [held.tile([P, PACK, QH], F32, name="q_raw%d" % h) for h in range(HALVES)]
+
+        g_rows = gT.rearrange("(p t) c -> p t c", t=PACK)
+        k_rows = kT.rearrange("(p t) c -> p t c", t=PACK)
+        q_rows = qT.rearrange("b (p t) c -> (b p) t c", t=PACK)
+
+        nc.sync.dma_start(gates[0][:], g_rows[:, 0, :])
+        nc.sync.dma_start(gate_list[:], offs2)
+        nc.sync.dma_start(key_list[:], offs)
+        nc.sync.dma_start(th_cols[:], th.rearrange("a b (p c) -> (a b p) c", c=2))
+        for t in range(1, PACK):
+            nc.sync.dma_start(gates[t][:], g_rows[:, t, :])
+        for t in range(PACK):
+            nc.sync.dma_start(keys[t][:], k_rows[:, t, :])
+        for h in range(HALVES):
+            nc.sync.dma_start(q_raw[h][:], q_rows[:, :, h * QH : (h + 1) * QH])
+
+        ident = held.tile([P, P], F32, name="ident")
+        make_identity(nc, ident[:])
+        warm = held.tile([P, 1], F32, name="warm")
+        nc.scalar.activation(warm[:], ident[:, 0:1], SIGMOID)
+
+        th_psum = psum.tile([P, 2, P], F32, name="th_psum")
+        for c in range(2):
+            nc.tensor.transpose(th_psum[:, c, :], th_cols[:, c : c + 1].to_broadcast([P, P]), ident[:])
+        th_all = held.tile([P, NQ], F32, name="th_all")
+        nc.scalar.copy(th_all[:].rearrange("p (k c) -> p k c", c=2), th_psum[:].rearrange("p c k -> p k c"))
+
+        picked = [held.tile([P, SLOTS], F32, name="picked%d" % t) for t in range(PACK)]
+        for t in range(PACK):
+            nc.vector.tensor_copy(picked[t][:], gates[t][:].indirect(gate_list[:]))
+
+        u_pair = [held.tile([P, 2, SLOTS], F32, name="u_pair%d" % j) for j in range(2)]
+        u_bf = held.tile([P, PACK, P, PACK], BF16, name="u_bf", align_bytes=64)
+
+        def gate_keys(t):
+            nc.vector.tensor_tensor(u_pair[t // 2][:, t % 2, :], keys[t][:].indirect(key_list[:]), picked[t][:], MULT)
+
+        def weave_u(copy, j):
+            copy(
+                u_bf[:, :, :, 2 * j : 2 * j + 2].rearrange("p r s t -> p s t r"),
+                u_pair[j][:].rearrange("p t (s r) -> p s t r", r=PACK),
+            )
+
+        q_bf = [held.tile([P, QH, PACK], BF16, name="q_bf%d" % h, align_bytes=64) for h in range(HALVES)]
+        q_codes = [held.tile([P, QH], I32, name="q_codes%d" % h, align_bytes=64) for h in range(HALVES)]
+        q_scales = [held.tile([P, QH], U8, name="q_scales%d" % h, align_bytes=64) for h in range(HALVES)]
+
+        def weave_q(h):
+            nc.scalar.copy(
+                q_bf[h][:].rearrange("p (c i) t -> p c t i", i=4),
+                q_raw[h][:].rearrange("p t (c i) -> p c t i", i=4),
+            )
+
+        def quantize_q(h):
+            nc.vector.quantize_mx(q_codes[h][:].bitcast(FP8X4), q_scales[h][:], q_bf[h][:].rearrange("p c t -> p (c t)"))
+
+        gate_keys(0)
+        gate_keys(1)
+        weave_u(nc.scalar.copy, 0)
+        gate_keys(2)
+        gate_keys(3)
+        weave_q(0)
+        weave_q(1)
+        quantize_q(0)
+        weave_u(nc.vector.tensor_copy, 1)
+        quantize_q(1)
+
+        u_codes = [held.tile([P, P], I32, name="u_codes%d" % r, align_bytes=64) for r in range(PACK)]
+        u_scales = [held.tile([P, P], U8, name="u_scales%d" % r, align_bytes=64) for r in range(PACK)]
+        for r in range(PACK):
+            nc.vector.quantize_mx(u_codes[r][:].bitcast(FP8X4), u_scales[r][:], u_bf[:, r, :, :].rearrange("p s t -> p (s t)"))
+
+        y = [held.tile([P, PACK, QH], F32, name="y%d" % h) for h in range(HALVES)]
+        out_rows = out_0.rearrange("(p r) q -> p r q", r=PACK)
+        for h in range(HALVES):
+            cols = slice(h * QH, (h + 1) * QH)
+            for j in range(2):
+                acc = psum.tile([P, 2, QH], F32, name="acc%d%d" % (h, j))
+                for i in range(2):
+                    r = 2 * j + i
+                    nc.tensor.matmul_mx(
+                        acc[:, i, :],
+                        lhsT=u_codes[r][:].bitcast(FP8X4),
+                        lhsT_scale=u_scales[r][:],
+                        rhs=q_codes[h][:].bitcast(FP8X4),
+                        rhs_scale=q_scales[h][:],
+                        start=True,
+                        stop=True,
+                    )
+                z = held.tile([P, 2, QH], F32, name="z%d%d" % (h, j))
+                nc.vector.tensor_tensor(z[:], acc[:], th_all[:, cols].unsqueeze(1).to_broadcast([P, 2, QH]), SUBTRACT)
+                nc.scalar.activation(y[h][:, 2 * j : 2 * j + 2, :], z[:], SIGMOID)
+            nc.sync.dma_start(out_rows[:, :, cols], y[h][:])
+
+        y_bf = [held.tile([P, QH, PACK], BF16, name="y_bf%d" % h, align_bytes=64) for h in range(HALVES)]
+        y_codes = [held.tile([P, QH], I32, name="y_codes%d" % h, align_bytes=64) for h in range(HALVES)]
+        y_scales = held.tile([P, NQ], U8, name="y_scales", align_bytes=64)
+        words = out_1.rearrange("s p q x -> (s p) (q x)").bitcast(I32)
+        for h in range(HALVES):
+            nc.vector.tensor_copy(
+                y_bf[h][:].rearrange("p (c i) r -> p c r i", i=4),
+                y[h][:].rearrange("p r (c i) -> p c r i", i=4),
+            )
+        for h in range(HALVES):
+            cols = slice(h * QH, (h + 1) * QH)
+            nc.vector.quantize_mx(y_codes[h][:].bitcast(FP8X4), y_scales[:, cols], y_bf[h][:].rearrange("p c r -> p (c r)"))
+            nc.sync.dma_start(words[:, cols], y_codes[h][:])
+        scale_rows = out_2.rearrange("s f q -> (s f) q").bitcast(I32)
+        for quadrant in range(4):
+            queue = nc.scalar if quadrant % 2 == 0 else nc.sync
+            queue.dma_start(
+                scale_rows[4 * quadrant : 4 * quadrant + 4, :],
+                y_scales[32 * quadrant : 32 * quadrant + 4, :].bitcast(I32),
+            )

@@ -30,24 +30,22 @@ def tile_attend_plw_gatekey_f_topk_kernel(tc, qT, kT, gT, th, offs, offs2, out_0
         key_list = held.tile([P, SLOTS // 16], U16, name="key_list")
         gate_list = held.tile([P, SLOTS // 16], U16, name="gate_list")
         th_cols = held.tile([P, 2], F32, name="th_cols")
-        gates = [held.tile([P, GATES], F32, name="gates%d" % t) for t in range(PACK)]
+        gates = [held.tile([P, 2, GATES], F32, name="gates%d" % j) for j in range(2)]
         keys = [held.tile([P, TOKENS], F32, name="keys%d" % t) for t in range(PACK)]
-        q_raw = [held.tile([P, PACK, QH], F32, name="q_raw%d" % h) for h in range(HALVES)]
+        q_raw = held.tile([P, PACK, NQ], F32, name="q_raw", tag="q_then_u", align_bytes=64)
 
         g_rows = gT.rearrange("(p t) c -> p t c", t=PACK)
         k_rows = kT.rearrange("(p t) c -> p t c", t=PACK)
         q_rows = qT.rearrange("b (p t) c -> (b p) t c", t=PACK)
 
-        nc.sync.dma_start(gates[0][:], g_rows[:, 0, :])
+        nc.sync.dma_start(gates[0][:], g_rows[:, 0:2, :])
         nc.sync.dma_start(gate_list[:], offs2)
         nc.sync.dma_start(key_list[:], offs)
         nc.sync.dma_start(th_cols[:], th.rearrange("a b (p c) -> (a b p) c", c=2))
-        for t in range(1, PACK):
-            nc.sync.dma_start(gates[t][:], g_rows[:, t, :])
+        nc.sync.dma_start(gates[1][:], g_rows[:, 2:4, :])
         for t in range(PACK):
             nc.sync.dma_start(keys[t][:], k_rows[:, t, :])
-        for h in range(HALVES):
-            nc.sync.dma_start(q_raw[h][:], q_rows[:, :, h * QH : (h + 1) * QH])
+        nc.sync.dma_start(q_raw[:], q_rows)
 
         ident = held.tile([P, P], F32, name="ident")
         make_identity(nc, ident[:])
@@ -62,18 +60,23 @@ def tile_attend_plw_gatekey_f_topk_kernel(tc, qT, kT, gT, th, offs, offs2, out_0
 
         picked = [held.tile([P, SLOTS], F32, name="picked%d" % t) for t in range(PACK)]
         for t in range(PACK):
-            nc.vector.tensor_copy(picked[t][:], gates[t][:].indirect(gate_list[:]))
+            nc.vector.tensor_copy(picked[t][:], gates[t // 2][:, t % 2, :].indirect(gate_list[:]))
 
         u_pair = [held.tile([P, 2, SLOTS], F32, name="u_pair%d" % j) for j in range(2)]
         u_bf = held.tile([P, PACK, P, PACK], BF16, name="u_bf", align_bytes=64)
 
-        def gate_keys(t):
-            nc.vector.tensor_tensor(u_pair[t // 2][:, t % 2, :], keys[t][:].indirect(key_list[:]), picked[t][:], MULT)
+        def gate_keys(t, first, last):
+            nc.vector.tensor_tensor(
+                u_pair[t // 2][:, t % 2, first:last],
+                keys[t][:].indirect(key_list[:, first // 16 : last // 16]),
+                picked[t][:, first:last],
+                MULT,
+            )
 
-        def weave_u(copy, j):
+        def weave_u(copy, j, first, last):
             copy(
-                u_bf[:, :, :, 2 * j : 2 * j + 2].rearrange("p r s t -> p s t r"),
-                u_pair[j][:].rearrange("p t (s r) -> p s t r", r=PACK),
+                u_bf[:, :, first // PACK : last // PACK, 2 * j : 2 * j + 2].rearrange("p r s t -> p s t r"),
+                u_pair[j][:, :, first:last].rearrange("p t (s r) -> p s t r", r=PACK),
             )
 
         q_bf = [held.tile([P, QH, PACK], BF16, name="q_bf%d" % h, align_bytes=64) for h in range(HALVES)]
@@ -83,39 +86,44 @@ def tile_attend_plw_gatekey_f_topk_kernel(tc, qT, kT, gT, th, offs, offs2, out_0
         def weave_q(h):
             nc.scalar.copy(
                 q_bf[h][:].rearrange("p (c i) t -> p c t i", i=4),
-                q_raw[h][:].rearrange("p t (c i) -> p c t i", i=4),
+                q_raw[:, :, h * QH : (h + 1) * QH].rearrange("p t (c i) -> p c t i", i=4),
             )
 
         def quantize_q(h):
             nc.vector.quantize_mx(q_codes[h][:].bitcast(FP8X4), q_scales[h][:], q_bf[h][:].rearrange("p c t -> p (c t)"))
 
-        gate_keys(0)
-        gate_keys(1)
-        weave_u(nc.scalar.copy, 0)
-        gate_keys(2)
-        gate_keys(3)
+        gate_keys(0, 0, SLOTS)
+        gate_keys(1, 0, SLOTS)
+        weave_u(nc.scalar.copy, 0, 0, SLOTS)
+        gate_keys(2, 0, SLOTS)
+        gate_keys(3, 0, SLOTS // 2)
+        gate_keys(3, SLOTS // 2, SLOTS)
         weave_q(0)
         weave_q(1)
+        weave_u(nc.vector.tensor_copy, 1, 0, SLOTS // 2)
+        weave_u(nc.vector.tensor_copy, 1, SLOTS // 2, SLOTS)
         quantize_q(0)
-        weave_u(nc.vector.tensor_copy, 1)
-        quantize_q(1)
 
-        u_codes = [held.tile([P, P], I32, name="u_codes%d" % r, align_bytes=64) for r in range(PACK)]
+        u_all = held.tile([P, SLOTS], I32, name="u_all", tag="q_then_u", align_bytes=64)
+        u_codes = [u_all[:, r * P : (r + 1) * P] for r in range(PACK)]
         u_scales = [held.tile([P, P], U8, name="u_scales%d" % r, align_bytes=64) for r in range(PACK)]
         for r in range(PACK):
-            nc.vector.quantize_mx(u_codes[r][:].bitcast(FP8X4), u_scales[r][:], u_bf[:, r, :, :].rearrange("p s t -> p (s t)"))
+            nc.vector.quantize_mx(u_codes[r].bitcast(FP8X4), u_scales[r][:], u_bf[:, r, :, :].rearrange("p s t -> p (s t)"))
+        quantize_q(1)
 
         y = [held.tile([P, PACK, QH], F32, name="y%d" % h) for h in range(HALVES)]
+        y_bf = [held.tile([P, QH, PACK], BF16, name="y_bf%d" % h, align_bytes=64) for h in range(HALVES)]
         out_rows = out_0.rearrange("(p r) q -> p r q", r=PACK)
         for h in range(HALVES):
             cols = slice(h * QH, (h + 1) * QH)
             for j in range(2):
+                pair = slice(2 * j, 2 * j + 2)
                 acc = psum.tile([P, 2, QH], F32, name="acc%d%d" % (h, j))
                 for i in range(2):
                     r = 2 * j + i
                     nc.tensor.matmul_mx(
                         acc[:, i, :],
-                        lhsT=u_codes[r][:].bitcast(FP8X4),
+                        lhsT=u_codes[r].bitcast(FP8X4),
                         lhsT_scale=u_scales[r][:],
                         rhs=q_codes[h][:].bitcast(FP8X4),
                         rhs_scale=q_scales[h][:],
@@ -124,22 +132,30 @@ def tile_attend_plw_gatekey_f_topk_kernel(tc, qT, kT, gT, th, offs, offs2, out_0
                     )
                 z = held.tile([P, 2, QH], F32, name="z%d%d" % (h, j))
                 nc.vector.tensor_tensor(z[:], acc[:], th_all[:, cols].unsqueeze(1).to_broadcast([P, 2, QH]), SUBTRACT)
-                nc.scalar.activation(y[h][:, 2 * j : 2 * j + 2, :], z[:], SIGMOID)
-            nc.sync.dma_start(out_rows[:, :, cols], y[h][:])
+                if h == 1 and j == 1:
+                    nc.scalar.activation(y_bf[h][:, :, pair], z[:].rearrange("p r c -> p c r"), SIGMOID)
+                nc.scalar.activation(y[h][:, pair, :], z[:], SIGMOID)
+                if h == 1:
+                    queue = nc.scalar if j == 1 else nc.sync
+                    queue.dma_start(out_rows[:, pair, cols], y[h][:, pair, :])
+            if h == 0:
+                nc.sync.dma_start(out_rows[:, :, cols], y[h][:])
 
-        y_bf = [held.tile([P, QH, PACK], BF16, name="y_bf%d" % h, align_bytes=64) for h in range(HALVES)]
-        y_codes = [held.tile([P, QH], I32, name="y_codes%d" % h, align_bytes=64) for h in range(HALVES)]
+        y_codes = held.tile([P, NQ], I32, name="y_codes", align_bytes=64)
         y_scales = held.tile([P, NQ], U8, name="y_scales", align_bytes=64)
         words = out_1.rearrange("s p q x -> (s p) (q x)").bitcast(I32)
-        for h in range(HALVES):
-            nc.vector.tensor_copy(
-                y_bf[h][:].rearrange("p (c i) r -> p c r i", i=4),
-                y[h][:].rearrange("p r (c i) -> p c r i", i=4),
-            )
+        nc.vector.tensor_copy(
+            y_bf[0][:].rearrange("p (c i) r -> p c r i", i=4),
+            y[0][:].rearrange("p r (c i) -> p c r i", i=4),
+        )
+        nc.vector.tensor_copy(
+            y_bf[1][:, :, 0:2].rearrange("p (c i) r -> p c r i", i=4),
+            y[1][:, 0:2, :].rearrange("p r (c i) -> p c r i", i=4),
+        )
         for h in range(HALVES):
             cols = slice(h * QH, (h + 1) * QH)
-            nc.vector.quantize_mx(y_codes[h][:].bitcast(FP8X4), y_scales[:, cols], y_bf[h][:].rearrange("p c r -> p (c r)"))
-            nc.sync.dma_start(words[:, cols], y_codes[h][:])
+            nc.vector.quantize_mx(y_codes[:, cols].bitcast(FP8X4), y_scales[:, cols], y_bf[h][:].rearrange("p c r -> p (c r)"))
+        nc.sync.dma_start(words, y_codes[:])
         scale_rows = out_2.rearrange("s f q -> (s f) q").bitcast(I32)
         for quadrant in range(4):
             queue = nc.scalar if quadrant % 2 == 0 else nc.sync

@@ -30,7 +30,7 @@ def tile_attend_plw_gatekey_f_topk_kernel(tc, qT, kT, gT, th, offs, offs2, out_0
         key_list = held.tile([P, SLOTS // 16], U16, name="key_list")
         gate_list = held.tile([P, SLOTS // 16], U16, name="gate_list")
         th_cols = held.tile([P, 2], F32, name="th_cols")
-        gates = [held.tile([P, 2, GATES], F32, name="gates%d" % j) for j in range(2)]
+        gates = [held.tile([P, GATES], F32, name="gates%d" % t) for t in range(PACK)]
         keys = [held.tile([P, TOKENS], F32, name="keys%d" % t) for t in range(PACK)]
         q_raw = held.tile([P, PACK, NQ], F32, name="q_raw", tag="q_then_u", align_bytes=64)
 
@@ -38,11 +38,12 @@ def tile_attend_plw_gatekey_f_topk_kernel(tc, qT, kT, gT, th, offs, offs2, out_0
         k_rows = kT.rearrange("(p t) c -> p t c", t=PACK)
         q_rows = qT.rearrange("b (p t) c -> (b p) t c", t=PACK)
 
-        nc.sync.dma_start(gates[0][:], g_rows[:, 0:2, :])
+        nc.sync.dma_start(gates[0][:], g_rows[:, 0, :])
         nc.sync.dma_start(gate_list[:], offs2)
         nc.sync.dma_start(key_list[:], offs)
         nc.sync.dma_start(th_cols[:], th.rearrange("a b (p c) -> (a b p) c", c=2))
-        nc.sync.dma_start(gates[1][:], g_rows[:, 2:4, :])
+        for t in range(1, PACK):
+            nc.sync.dma_start(gates[t][:], g_rows[:, t, :])
         for t in range(PACK):
             nc.sync.dma_start(keys[t][:], k_rows[:, t, :])
         nc.sync.dma_start(q_raw[:], q_rows)
@@ -60,7 +61,7 @@ def tile_attend_plw_gatekey_f_topk_kernel(tc, qT, kT, gT, th, offs, offs2, out_0
 
         picked = [held.tile([P, SLOTS], F32, name="picked%d" % t) for t in range(PACK)]
         for t in range(PACK):
-            nc.vector.tensor_copy(picked[t][:], gates[t // 2][:, t % 2, :].indirect(gate_list[:]))
+            nc.vector.tensor_copy(picked[t][:], gates[t][:].indirect(gate_list[:]))
 
         u_pair = [held.tile([P, 2, SLOTS], F32, name="u_pair%d" % j) for j in range(2)]
         u_bf = held.tile([P, PACK, P, PACK], BF16, name="u_bf", align_bytes=64)
@@ -75,8 +76,8 @@ def tile_attend_plw_gatekey_f_topk_kernel(tc, qT, kT, gT, th, offs, offs2, out_0
 
         def weave_u(copy, j, first, last):
             copy(
-                u_bf[:, :, first // PACK : last // PACK, 2 * j : 2 * j + 2].rearrange("p r s t -> p s t r"),
-                u_pair[j][:, :, first:last].rearrange("p t (s r) -> p s t r", r=PACK),
+                u_bf[:, :, first // PACK : last // PACK, 2 * j : 2 * j + 2].rearrange("p (a b) s t -> p a s t b", b=2),
+                u_pair[j][:, :, first:last].rearrange("p t (s a b) -> p a s t b", a=2, b=2),
             )
 
         q_bf = [held.tile([P, QH, PACK], BF16, name="q_bf%d" % h, align_bytes=64) for h in range(HALVES)]
@@ -109,15 +110,16 @@ def tile_attend_plw_gatekey_f_topk_kernel(tc, qT, kT, gT, th, offs, offs2, out_0
         u_scales = [held.tile([P, P], U8, name="u_scales%d" % r, align_bytes=64) for r in range(PACK)]
         for r in range(PACK):
             nc.vector.quantize_mx(u_codes[r].bitcast(FP8X4), u_scales[r][:], u_bf[:, r, :, :].rearrange("p s t -> p (s t)"))
-        quantize_q(1)
+            if r == 1:
+                quantize_q(1)
 
-        y = [held.tile([P, PACK, QH], F32, name="y%d" % h) for h in range(HALVES)]
+        y = held.tile([P, PACK, NQ], F32, name="y")
         y_bf = [held.tile([P, QH, PACK], BF16, name="y_bf%d" % h, align_bytes=64) for h in range(HALVES)]
         out_rows = out_0.rearrange("(p r) q -> p r q", r=PACK)
-        for h in range(HALVES):
-            cols = slice(h * QH, (h + 1) * QH)
-            for j in range(2):
-                pair = slice(2 * j, 2 * j + 2)
+        for j in range(2):
+            pair = slice(2 * j, 2 * j + 2)
+            for h in range(HALVES):
+                cols = slice(h * QH, (h + 1) * QH)
                 acc = psum.tile([P, 2, QH], F32, name="acc%d%d" % (h, j))
                 for i in range(2):
                     r = 2 * j + i
@@ -132,30 +134,21 @@ def tile_attend_plw_gatekey_f_topk_kernel(tc, qT, kT, gT, th, offs, offs2, out_0
                     )
                 z = held.tile([P, 2, QH], F32, name="z%d%d" % (h, j))
                 nc.vector.tensor_tensor(z[:], acc[:], th_all[:, cols].unsqueeze(1).to_broadcast([P, 2, QH]), SUBTRACT)
-                if h == 1 and j == 1:
-                    nc.scalar.activation(y_bf[h][:, :, pair], z[:].rearrange("p r c -> p c r"), SIGMOID)
-                nc.scalar.activation(y[h][:, pair, :], z[:], SIGMOID)
-                if h == 1:
-                    queue = nc.scalar if j == 1 else nc.sync
-                    queue.dma_start(out_rows[:, pair, cols], y[h][:, pair, :])
-            if h == 0:
-                nc.sync.dma_start(out_rows[:, :, cols], y[h][:])
+                nc.scalar.activation(y[:, pair, cols], z[:], SIGMOID)
+            nc.sync.dma_start(out_rows[:, pair, :], y[:, pair, :])
 
         y_codes = held.tile([P, NQ], I32, name="y_codes", align_bytes=64)
         y_scales = held.tile([P, NQ], U8, name="y_scales", align_bytes=64)
         words = out_1.rearrange("s p q x -> (s p) (q x)").bitcast(I32)
-        nc.vector.tensor_copy(
-            y_bf[0][:].rearrange("p (c i) r -> p c r i", i=4),
-            y[0][:].rearrange("p r (c i) -> p c r i", i=4),
-        )
-        nc.vector.tensor_copy(
-            y_bf[1][:, :, 0:2].rearrange("p (c i) r -> p c r i", i=4),
-            y[1][:, 0:2, :].rearrange("p r (c i) -> p c r i", i=4),
-        )
+        for h in range(HALVES):
+            nc.vector.tensor_copy(
+                y_bf[h][:].rearrange("p (c i) r -> p c r i", i=4),
+                y[:, :, h * QH : (h + 1) * QH].rearrange("p r (c i) -> p c r i", i=4),
+            )
         for h in range(HALVES):
             cols = slice(h * QH, (h + 1) * QH)
             nc.vector.quantize_mx(y_codes[:, cols].bitcast(FP8X4), y_scales[:, cols], y_bf[h][:].rearrange("p c r -> p (c r)"))
-        nc.sync.dma_start(words, y_codes[:])
+            nc.sync.dma_start(words[:, cols], y_codes[:, cols])
         scale_rows = out_2.rearrange("s f q -> (s f) q").bitcast(I32)
         for quadrant in range(4):
             queue = nc.scalar if quadrant % 2 == 0 else nc.sync

@@ -30,7 +30,7 @@ def tile_attend_plw_gatekey_f_topk_kernel(tc, qT, kT, gT, th, offs, offs2, out_0
         key_list = held.tile([P, SLOTS // 16], U16, name="key_list")
         gate_list = held.tile([P, SLOTS // 16], U16, name="gate_list")
         th_cols = held.tile([P, 2], F32, name="th_cols")
-        gates = [held.tile([P, GATES], F32, name="gates%d" % t) for t in range(PACK)]
+        gates = [held.tile([P, 2, GATES], F32, name="gates%d" % j) for j in range(2)]
         keys = [held.tile([P, TOKENS], F32, name="keys%d" % t) for t in range(PACK)]
         q_raw = held.tile([P, PACK, NQ], F32, name="q_raw", tag="q_then_u", align_bytes=64)
 
@@ -38,12 +38,11 @@ def tile_attend_plw_gatekey_f_topk_kernel(tc, qT, kT, gT, th, offs, offs2, out_0
         k_rows = kT.rearrange("(p t) c -> p t c", t=PACK)
         q_rows = qT.rearrange("b (p t) c -> (b p) t c", t=PACK)
 
-        nc.sync.dma_start(gates[0][:], g_rows[:, 0, :])
+        nc.sync.dma_start(gates[0][:], g_rows[:, 0:2, :])
         nc.sync.dma_start(gate_list[:], offs2)
         nc.sync.dma_start(key_list[:], offs)
         nc.sync.dma_start(th_cols[:], th.rearrange("a b (p c) -> (a b p) c", c=2))
-        for t in range(1, PACK):
-            nc.sync.dma_start(gates[t][:], g_rows[:, t, :])
+        nc.sync.dma_start(gates[1][:], g_rows[:, 2:4, :])
         for t in range(PACK):
             nc.sync.dma_start(keys[t][:], k_rows[:, t, :])
         nc.sync.dma_start(q_raw[:], q_rows)
@@ -61,7 +60,7 @@ def tile_attend_plw_gatekey_f_topk_kernel(tc, qT, kT, gT, th, offs, offs2, out_0
 
         picked = [held.tile([P, SLOTS], F32, name="picked%d" % t) for t in range(PACK)]
         for t in range(PACK):
-            nc.vector.tensor_copy(picked[t][:], gates[t][:].indirect(gate_list[:]))
+            nc.vector.tensor_copy(picked[t][:], gates[t // 2][:, t % 2, :].indirect(gate_list[:]))
 
         u_pair = [held.tile([P, 2, SLOTS], F32, name="u_pair%d" % j) for j in range(2)]
         u_bf = held.tile([P, PACK, P, PACK], BF16, name="u_bf", align_bytes=64)
@@ -116,28 +115,33 @@ def tile_attend_plw_gatekey_f_topk_kernel(tc, qT, kT, gT, th, offs, offs2, out_0
         y = held.tile([P, PACK, NQ], F32, name="y")
         y_bf = [held.tile([P, QH, PACK], BF16, name="y_bf%d" % h, align_bytes=64) for h in range(HALVES)]
         out_rows = out_0.rearrange("(p r) q -> p r q", r=PACK)
-        for j in range(2):
-            pair = slice(2 * j, 2 * j + 2)
-            for h in range(HALVES):
-                cols = slice(h * QH, (h + 1) * QH)
-                acc = psum.tile([P, 2, QH], F32, name="acc%d%d" % (h, j))
-                for i in range(2):
-                    r = 2 * j + i
-                    nc.tensor.matmul_mx(
-                        acc[:, i, :],
-                        lhsT=u_codes[r].bitcast(FP8X4),
-                        lhsT_scale=u_scales[r][:],
-                        rhs=q_codes[h][:].bitcast(FP8X4),
-                        rhs_scale=q_scales[h][:],
-                        start=True,
-                        stop=True,
-                    )
-                z = held.tile([P, 2, QH], F32, name="z%d%d" % (h, j))
-                nc.vector.tensor_tensor(z[:], acc[:], th_all[:, cols].unsqueeze(1).to_broadcast([P, 2, QH]), SUBTRACT)
-                nc.scalar.activation(y[:, pair, cols], z[:], SIGMOID)
-            nc.sync.dma_start(out_rows[:, pair, :], y[:, pair, :])
 
-        y_codes = held.tile([P, NQ], I32, name="y_codes", align_bytes=64)
+        def score(first, count, h):
+            cols = slice(h * QH, (h + 1) * QH)
+            acc = psum.tile([P, count, QH], F32, name="acc%d%d" % (h, first))
+            for i in range(count):
+                nc.tensor.matmul_mx(
+                    acc[:, i, :],
+                    lhsT=u_codes[first + i].bitcast(FP8X4),
+                    lhsT_scale=u_scales[first + i][:],
+                    rhs=q_codes[h][:].bitcast(FP8X4),
+                    rhs_scale=q_scales[h][:],
+                    start=True,
+                    stop=True,
+                )
+            z = held.tile([P, count, QH], F32, name="z%d%d" % (h, first), tag="z%d%d" % (h, first), align_bytes=64)
+            nc.vector.tensor_tensor(z[:], acc[:], th_all[:, cols].unsqueeze(1).to_broadcast([P, count, QH]), SUBTRACT)
+            nc.scalar.activation(y[:, first : first + count, cols], z[:], SIGMOID)
+
+        score(0, 2, 0)
+        score(0, 2, 1)
+        nc.sync.dma_start(out_rows[:, 0:2, :], y[:, 0:2, :])
+        score(2, 2, 0)
+        score(2, 1, 1)
+        score(3, 1, 1)
+        nc.sync.dma_start(out_rows[:, 2:4, :], y[:, 2:4, :])
+
+        y_codes = held.tile([P, NQ], I32, name="y_codes", tag="z13", align_bytes=64)
         y_scales = held.tile([P, NQ], U8, name="y_scales", align_bytes=64)
         words = out_1.rearrange("s p q x -> (s p) (q x)").bitcast(I32)
         for h in range(HALVES):

@@ -109,15 +109,13 @@ def tile_attend_plw_gatekey_f_topk_kernel(tc, qT, kT, gT, th, offs, offs2, out_0
         u_scales = [held.tile([P, P], U8, name="u_scales%d" % r, align_bytes=64) for r in range(PACK)]
         for r in range(PACK):
             nc.vector.quantize_mx(u_codes[r].bitcast(FP8X4), u_scales[r][:], u_bf[:, r, :, :].rearrange("p s t -> p (s t)"))
-            if r == 1:
-                quantize_q(1)
+        quantize_q(1)
 
         y = held.tile([P, PACK, NQ], F32, name="y")
         y_bf = [held.tile([P, QH, PACK], BF16, name="y_bf%d" % h, align_bytes=64) for h in range(HALVES)]
         out_rows = out_0.rearrange("(p r) q -> p r q", r=PACK)
 
-        def score(first, count, h):
-            cols = slice(h * QH, (h + 1) * QH)
+        def score(first, count, h, pieces=1):
             acc = psum.tile([P, count, QH], F32, name="acc%d%d" % (h, first))
             for i in range(count):
                 nc.tensor.matmul_mx(
@@ -129,30 +127,48 @@ def tile_attend_plw_gatekey_f_topk_kernel(tc, qT, kT, gT, th, offs, offs2, out_0
                     start=True,
                     stop=True,
                 )
-            z = held.tile([P, count, QH], F32, name="z%d%d" % (h, first), tag="z%d%d" % (h, first), align_bytes=64)
-            nc.vector.tensor_tensor(z[:], acc[:], th_all[:, cols].unsqueeze(1).to_broadcast([P, count, QH]), SUBTRACT)
-            nc.scalar.activation(y[:, first : first + count, cols], z[:], SIGMOID)
+            width = QH // pieces
+            for k in range(pieces):
+                cols = slice(h * QH + k * width, h * QH + (k + 1) * width)
+                tag = "z%d%d%d" % (h, first, k)
+                z = held.tile([P, count, width], F32, name=tag, tag=tag, align_bytes=64)
+                nc.vector.tensor_tensor(
+                    z[:],
+                    acc[:, :, k * width : (k + 1) * width],
+                    th_all[:, cols].unsqueeze(1).to_broadcast([P, count, width]),
+                    SUBTRACT,
+                )
+                nc.scalar.activation(y[:, first : first + count, cols], z[:], SIGMOID)
 
         score(0, 2, 0)
-        score(0, 2, 1)
-        nc.sync.dma_start(out_rows[:, 0:2, :], y[:, 0:2, :])
         score(2, 2, 0)
+        score(0, 1, 1)
+        nc.sync.dma_start(out_rows[:, 0, :], y[:, 0, :])
+        score(1, 1, 1)
         score(2, 1, 1)
-        score(3, 1, 1)
-        nc.sync.dma_start(out_rows[:, 2:4, :], y[:, 2:4, :])
+        nc.sync.dma_start(out_rows[:, 1:3, :], y[:, 1:3, :])
+        score(3, 1, 1, 2)
+        nc.sync.dma_start(out_rows[:, 3, :], y[:, 3, :])
 
-        y_codes = held.tile([P, NQ], I32, name="y_codes", tag="z13", align_bytes=64)
+        y_codes = held.tile([P, NQ], I32, name="y_codes", align_bytes=64)
         y_scales = held.tile([P, NQ], U8, name="y_scales", align_bytes=64)
         words = out_1.rearrange("s p q x -> (s p) (q x)").bitcast(I32)
-        for h in range(HALVES):
+        for h, first, last in ((0, 0, QH), (1, 0, QH // 2), (1, QH // 2, QH)):
             nc.vector.tensor_copy(
-                y_bf[h][:].rearrange("p (c i) r -> p c r i", i=4),
-                y[:, :, h * QH : (h + 1) * QH].rearrange("p r (c i) -> p c r i", i=4),
+                y_bf[h][:, first:last, :].rearrange("p (c i) r -> p c r i", i=4),
+                y[:, :, h * QH + first : h * QH + last].rearrange("p r (c i) -> p c r i", i=4),
             )
         for h in range(HALVES):
             cols = slice(h * QH, (h + 1) * QH)
-            nc.vector.quantize_mx(y_codes[:, cols].bitcast(FP8X4), y_scales[:, cols], y_bf[h][:].rearrange("p c r -> p (c r)"))
-            nc.sync.dma_start(words[:, cols], y_codes[:, cols])
+            width = QH // (h + 1)
+            for first in range(0, QH, width):
+                part = slice(h * QH + first, h * QH + first + width)
+                nc.vector.quantize_mx(
+                    y_codes[:, part].bitcast(FP8X4),
+                    y_scales[:, part],
+                    y_bf[h][:, first : first + width, :].rearrange("p c r -> p (c r)"),
+                )
+        nc.sync.dma_start(words, y_codes[:])
         scale_rows = out_2.rearrange("s f q -> (s f) q").bitcast(I32)
         for quadrant in range(4):
             queue = nc.scalar if quadrant % 2 == 0 else nc.sync

@@ -49,8 +49,6 @@ def tile_attend_plw_gatekey_f_topk_kernel(tc, qT, kT, gT, th, offs, offs2, out_0
 
         ident = held.tile([P, P], F32, name="ident")
         make_identity(nc, ident[:])
-        warm = held.tile([P, 1], F32, name="warm")
-        nc.scalar.activation(warm[:], ident[:, 0:1], SIGMOID)
 
         th_psum = psum.tile([P, 2, P], F32, name="th_psum")
         for c in range(2):

@@ -32,7 +32,7 @@ def tile_attend_plw_gatekey_f_topk_kernel(tc, qT, kT, gT, th, offs, offs2, out_0
         th_cols = held.tile([P, 2], F32, name="th_cols")
         gates = [held.tile([P, 2, GATES], F32, name="gates%d" % j) for j in range(2)]
         keys = [held.tile([P, TOKENS], F32, name="keys%d" % t) for t in range(PACK)]
-        q_raw = held.tile([P, PACK, NQ], F32, name="q_raw", tag="q_then_u", align_bytes=64)
+        q_raw = held.tile([P, PACK, NQ], F32, name="q_raw", align_bytes=64)
 
         g_rows = gT.rearrange("(p t) c -> p t c", t=PACK)
         k_rows = kT.rearrange("(p t) c -> p t c", t=PACK)
@@ -49,6 +49,9 @@ def tile_attend_plw_gatekey_f_topk_kernel(tc, qT, kT, gT, th, offs, offs2, out_0
 
         ident = held.tile([P, P], F32, name="ident")
         make_identity(nc, ident[:])
+
+        warm = held.tile([P, 1], F32, name="warm")
+        nc.scalar.activation(warm[:], ident[:, 0:1], SIGMOID)
 
         th_psum = psum.tile([P, 2, P], F32, name="th_psum")
         for c in range(2):
@@ -77,12 +80,12 @@ def tile_attend_plw_gatekey_f_topk_kernel(tc, qT, kT, gT, th, offs, offs2, out_0
                 u_pair[j][:, :, first:last].rearrange("p t (s a b) -> p a s t b", a=2, b=2),
             )
 
-        q_bf = [held.tile([P, QH, PACK], BF16, name="q_bf%d" % h, align_bytes=64) for h in range(HALVES)]
+        q_bf = [held.tile([P, QH, PACK], BF16, name="q_bf%d" % h, tag="q_bf%d" % h, align_bytes=64) for h in range(HALVES)]
         q_codes = [held.tile([P, QH], I32, name="q_codes%d" % h, align_bytes=64) for h in range(HALVES)]
         q_scales = [held.tile([P, QH], U8, name="q_scales%d" % h, align_bytes=64) for h in range(HALVES)]
 
-        def weave_q(h):
-            nc.scalar.copy(
+        def weave_q(copy, h):
+            copy(
                 q_bf[h][:].rearrange("p (c i) t -> p c t i", i=4),
                 q_raw[:, :, h * QH : (h + 1) * QH].rearrange("p t (c i) -> p c t i", i=4),
             )
@@ -94,15 +97,17 @@ def tile_attend_plw_gatekey_f_topk_kernel(tc, qT, kT, gT, th, offs, offs2, out_0
         gate_keys(1, 0, SLOTS)
         weave_u(nc.scalar.copy, 0, 0, SLOTS)
         gate_keys(2, 0, SLOTS)
-        gate_keys(3, 0, SLOTS // 2)
-        gate_keys(3, SLOTS // 2, SLOTS)
-        weave_q(0)
-        weave_q(1)
-        weave_u(nc.vector.tensor_copy, 1, 0, SLOTS // 2)
-        weave_u(nc.vector.tensor_copy, 1, SLOTS // 2, SLOTS)
+        cuts = (0, 128, 320, SLOTS)
+        for first, last in zip(cuts, cuts[1:]):
+            gate_keys(3, first, last)
+        weave_u(nc.scalar.copy, 1, cuts[0], cuts[1])
+        weave_q(nc.scalar.copy, 0)
+        weave_q(nc.scalar.copy, 1)
+        weave_u(nc.vector.tensor_copy, 1, cuts[1], cuts[2])
+        weave_u(nc.vector.tensor_copy, 1, cuts[2], cuts[3])
         quantize_q(0)
 
-        u_all = held.tile([P, SLOTS], I32, name="u_all", tag="q_then_u", align_bytes=64)
+        u_all = held.tile([P, SLOTS], I32, name="u_all", tag="q_bf0", align_bytes=64)
         u_codes = [u_all[:, r * P : (r + 1) * P] for r in range(PACK)]
         u_scales = [held.tile([P, P], U8, name="u_scales%d" % r, align_bytes=64) for r in range(PACK)]
         for r in range(PACK):

@@ -53,7 +53,7 @@ def tile_attend_plw_gatekey_f_topk_kernel(tc, qT, kT, gT, th, offs, offs2, out_0
         warm = held.tile([P, 1], F32, name="warm")
         nc.scalar.activation(warm[:], ident[:, 0:1], SIGMOID)
 
-        th_psum = psum.tile([P, 2, P], F32, name="th_psum")
+        th_psum = psum.tile([P, 2, P], F32, name="th_psum", tag="acc13")
         for c in range(2):
             nc.tensor.transpose(th_psum[:, c, :], th_cols[:, c : c + 1].to_broadcast([P, P]), ident[:])
         th_all = held.tile([P, NQ], F32, name="th_all")
@@ -114,65 +114,79 @@ def tile_attend_plw_gatekey_f_topk_kernel(tc, qT, kT, gT, th, offs, offs2, out_0
             nc.vector.quantize_mx(u_codes[r].bitcast(FP8X4), u_scales[r][:], u_bf[:, r, :, :].rearrange("p s t -> p (s t)"))
         quantize_q(1)
 
-        y = held.tile([P, PACK, NQ], F32, name="y")
-        y_bf = [held.tile([P, QH, PACK], BF16, name="y_bf%d" % h, align_bytes=64) for h in range(HALVES)]
-        out_rows = out_0.rearrange("(p r) q -> p r q", r=PACK)
-
-        def score(first, count, h, pieces=1):
-            acc = psum.tile([P, count, QH], F32, name="acc%d%d" % (h, first))
-            for i in range(count):
-                nc.tensor.matmul_mx(
-                    acc[:, i, :],
-                    lhsT=u_codes[first + i].bitcast(FP8X4),
-                    lhsT_scale=u_scales[first + i][:],
-                    rhs=q_codes[h][:].bitcast(FP8X4),
-                    rhs_scale=q_scales[h][:],
-                    start=True,
-                    stop=True,
-                )
-            width = QH // pieces
-            for k in range(pieces):
-                cols = slice(h * QH + k * width, h * QH + (k + 1) * width)
-                tag = "z%d%d%d" % (h, first, k)
-                z = held.tile([P, count, width], F32, name=tag, tag=tag, align_bytes=64)
-                nc.vector.tensor_tensor(
-                    z[:],
-                    acc[:, :, k * width : (k + 1) * width],
-                    th_all[:, cols].unsqueeze(1).to_broadcast([P, count, width]),
-                    SUBTRACT,
-                )
-                nc.scalar.activation(y[:, first : first + count, cols], z[:], SIGMOID)
-
-        score(0, 2, 0)
-        score(2, 2, 0)
-        score(0, 1, 1)
-        nc.sync.dma_start(out_rows[:, 0, :], y[:, 0, :])
-        score(1, 1, 1)
-        score(2, 1, 1)
-        nc.sync.dma_start(out_rows[:, 1:3, :], y[:, 1:3, :])
-        score(3, 1, 1, 2)
-        nc.sync.dma_start(out_rows[:, 3, :], y[:, 3, :])
-
+        z = held.tile([P, PACK, NQ], F32, name="z", align_bytes=64)
+        y = held.tile([P, PACK, NQ], F32, name="y", align_bytes=64)
+        y_bf = held.tile([P, NQ, PACK], BF16, name="y_bf", align_bytes=64)
         y_codes = held.tile([P, NQ], I32, name="y_codes", align_bytes=64)
         y_scales = held.tile([P, NQ], U8, name="y_scales", align_bytes=64)
+        out_rows = out_0.rearrange("(p r) q -> p r q", r=PACK)
         words = out_1.rearrange("s p q x -> (s p) (q x)").bitcast(I32)
-        for h, first, last in ((0, 0, QH), (1, 0, QH // 2), (1, QH // 2, QH)):
-            nc.vector.tensor_copy(
-                y_bf[h][:, first:last, :].rearrange("p (c i) r -> p c r i", i=4),
-                y[:, :, h * QH + first : h * QH + last].rearrange("p r (c i) -> p c r i", i=4),
-            )
-        for h in range(HALVES):
-            cols = slice(h * QH, (h + 1) * QH)
-            width = QH // (h + 1)
-            for first in range(0, QH, width):
-                part = slice(h * QH + first, h * QH + first + width)
-                nc.vector.quantize_mx(
-                    y_codes[:, part].bitcast(FP8X4),
-                    y_scales[:, part],
-                    y_bf[h][:, first : first + width, :].rearrange("p c r -> p (c r)"),
-                )
-        nc.sync.dma_start(words, y_codes[:])
         scale_rows = out_2.rearrange("s f q -> (s f) q").bitcast(I32)
+        acc = {}
+
+        def multiply(r, h):
+            acc[r, h] = psum.tile([P, QH], F32, name="acc%d%d" % (h, r), tag="acc%d%d" % (h, r))
+            nc.tensor.matmul_mx(
+                acc[r, h][:],
+                lhsT=u_codes[r].bitcast(FP8X4),
+                lhsT_scale=u_scales[r][:],
+                rhs=q_codes[h][:].bitcast(FP8X4),
+                rhs_scale=q_scales[h][:],
+                start=True,
+                stop=True,
+            )
+
+        def subtract(r, first, last):
+            h = first // QH
+            nc.vector.tensor_tensor(z[:, r, first:last], acc[r, h][:, first - h * QH : last - h * QH], th_all[:, first:last], SUBTRACT)
+
+        def sigmoid(r, first, last):
+            nc.scalar.activation(y[:, r, first:last], z[:, r, first:last], SIGMOID)
+
+        def score(r, h):
+            multiply(r, h)
+            subtract(r, h * QH, (h + 1) * QH)
+            sigmoid(r, h * QH, (h + 1) * QH)
+
+        def woven(first, last):
+            return y_bf[:, first:last, :].rearrange("p (c i) r -> p c r i", i=4)
+
+        def by_tile(src, first, last):
+            return src[:, :, first:last].rearrange("p r (c i) -> p c r i", i=4)
+
+        def weave_y(first, last):
+            nc.vector.tensor_copy(woven(first, last), by_tile(y, first, last))
+
+        def quantize_y(first, last):
+            nc.vector.quantize_mx(
+                y_codes[:, first:last].bitcast(FP8X4),
+                y_scales[:, first:last],
+                y_bf[:, first:last, :].rearrange("p c r -> p (c r)"),
+            )
+
+        def store_rows(first, last):
+            nc.sync.dma_start(out_rows[:, first:last, :], y[:, first:last, :])
+
+        for r in range(PACK):
+            score(r, 0)
+        score(0, 1)
+        store_rows(0, 1)
+        score(1, 1)
+        score(2, 1)
+        store_rows(1, 3)
+        multiply(3, 1)
+        subtract(3, 128, 192)
+        subtract(3, 192, 256)
+        sigmoid(3, 128, 192)
+        nc.scalar.activation(woven(192, 256), by_tile(z, 192, 256), SIGMOID)
+        sigmoid(3, 192, 256)
+        store_rows(3, 4)
+        weave_y(0, 128)
+        weave_y(128, 192)
+        quantize_y(0, 128)
+        quantize_y(128, 192)
+        quantize_y(192, 256)
+        nc.sync.dma_start(words, y_codes[:])
         for quadrant in range(4):
             queue = nc.scalar if quadrant % 2 == 0 else nc.sync
             queue.dma_start(

@@ -53,7 +53,7 @@ def tile_attend_plw_gatekey_f_topk_kernel(tc, qT, kT, gT, th, offs, offs2, out_0
         warm = held.tile([P, 1], F32, name="warm")
         nc.scalar.activation(warm[:], ident[:, 0:1], SIGMOID)
 
-        th_psum = psum.tile([P, 2, P], F32, name="th_psum", tag="acc13")
+        th_psum = psum.tile([P, 2, P], F32, name="th_psum", tag="acc11")
         for c in range(2):
             nc.tensor.transpose(th_psum[:, c, :], th_cols[:, c : c + 1].to_broadcast([P, P]), ident[:])
         th_all = held.tile([P, NQ], F32, name="th_all")
@@ -167,25 +167,34 @@ def tile_attend_plw_gatekey_f_topk_kernel(tc, qT, kT, gT, th, offs, offs2, out_0
         def store_rows(first, last):
             nc.sync.dma_start(out_rows[:, first:last, :], y[:, first:last, :])
 
-        for r in range(PACK):
-            score(r, 0)
-        score(0, 1)
-        store_rows(0, 1)
-        score(1, 1)
+        def woven_pair(j, first, last):
+            return y_bf[:, first:last, 2 * j : 2 * j + 2].rearrange("p (c i) r -> p c r i", i=4)
+
+        def pair_of(src, j, first, last):
+            return src[:, 2 * j : 2 * j + 2, first:last].rearrange("p r (c i) -> p c r i", i=4)
+
+        score(0, 0)
+        score(1, 0)
+        nc.sync.dma_start(out_rows[:, 0:2, 0:QH], y[:, 0:2, 0:QH])
+        score(2, 0)
+        score(3, 0)
         score(2, 1)
-        store_rows(1, 3)
-        multiply(3, 1)
-        subtract(3, 128, 192)
-        subtract(3, 192, 256)
-        sigmoid(3, 128, 192)
-        nc.scalar.activation(woven(192, 256), by_tile(z, 192, 256), SIGMOID)
-        sigmoid(3, 192, 256)
-        store_rows(3, 4)
+        score(3, 1)
+        store_rows(2, 4)
+        score(0, 1)
+        multiply(1, 1)
+        subtract(1, 128, 192)
+        subtract(1, 192, 256)
+        sigmoid(1, 128, 192)
+        nc.scalar.activation(woven_pair(0, 192, 256), pair_of(z, 0, 192, 256), SIGMOID)
+        sigmoid(1, 192, 256)
+        nc.sync.dma_start(out_rows[:, 0:2, QH:NQ], y[:, 0:2, QH:NQ])
         weave_y(0, 128)
+        nc.vector.tensor_copy(woven_pair(1, 192, 256), pair_of(y, 1, 192, 256))
         weave_y(128, 192)
         quantize_y(0, 128)
-        quantize_y(128, 192)
         quantize_y(192, 256)
+        quantize_y(128, 192)
         nc.sync.dma_start(words, y_codes[:])
         for quadrant in range(4):
             queue = nc.scalar if quadrant % 2 == 0 else nc.sync

@@ -80,6 +80,12 @@ def tile_attend_plw_gatekey_f_topk_kernel(tc, qT, kT, gT, th, offs, offs2, out_0
                 u_pair[j][:, :, first:last].rearrange("p t (s a b) -> p a s t b", a=2, b=2),
             )
 
+        def weave_u_tiles(copy, j, a, first, last):
+            copy(
+                u_bf[:, 2 * a : 2 * a + 2, first // PACK : last // PACK, 2 * j : 2 * j + 2].rearrange("p b s t -> p s t b"),
+                u_pair[j][:, :, first:last].rearrange("p t (s a b) -> p a s t b", a=2, b=2)[:, a],
+            )
+
         q_bf = [held.tile([P, QH, PACK], BF16, name="q_bf%d" % h, tag="q_bf%d" % h, align_bytes=64) for h in range(HALVES)]
         q_codes = [held.tile([P, QH], I32, name="q_codes%d" % h, align_bytes=64) for h in range(HALVES)]
         q_scales = [held.tile([P, QH], U8, name="q_scales%d" % h, align_bytes=64) for h in range(HALVES)]
@@ -97,14 +103,15 @@ def tile_attend_plw_gatekey_f_topk_kernel(tc, qT, kT, gT, th, offs, offs2, out_0
         gate_keys(1, 0, SLOTS)
         weave_u(nc.scalar.copy, 0, 0, SLOTS)
         gate_keys(2, 0, SLOTS)
-        cuts = (0, 128, 320, SLOTS)
+        cuts = (0, 128, 384, SLOTS)
         for first, last in zip(cuts, cuts[1:]):
             gate_keys(3, first, last)
         weave_u(nc.scalar.copy, 1, cuts[0], cuts[1])
         weave_q(nc.scalar.copy, 0)
         weave_q(nc.scalar.copy, 1)
         weave_u(nc.vector.tensor_copy, 1, cuts[1], cuts[2])
-        weave_u(nc.vector.tensor_copy, 1, cuts[2], cuts[3])
+        weave_u_tiles(nc.vector.tensor_copy, 1, 0, cuts[2], cuts[3])
+        weave_u_tiles(nc.vector.tensor_copy, 1, 1, cuts[2], cuts[3])
         quantize_q(0)
 
         u_all = held.tile([P, SLOTS], I32, name="u_all", tag="q_bf0", align_bytes=64)
@@ -181,13 +188,14 @@ def tile_attend_plw_gatekey_f_topk_kernel(tc, qT, kT, gT, th, offs, offs2, out_0
         score(2, 1)
         score(3, 1)
         store_rows(2, 4)
-        score(0, 1)
+        multiply(0, 1)
+        subtract(0, 128, 256)
         multiply(1, 1)
         subtract(1, 128, 192)
         subtract(1, 192, 256)
-        sigmoid(1, 128, 192)
+        nc.scalar.activation(y[:, 0:2, 128:192], z[:, 0:2, 128:192], SIGMOID)
         nc.scalar.activation(woven_pair(0, 192, 256), pair_of(z, 0, 192, 256), SIGMOID)
-        sigmoid(1, 192, 256)
+        nc.scalar.activation(y[:, 0:2, 192:256], z[:, 0:2, 192:256], SIGMOID)
         nc.sync.dma_start(out_rows[:, 0:2, QH:NQ], y[:, 0:2, QH:NQ])
         weave_y(0, 128)
         nc.vector.tensor_copy(woven_pair(1, 192, 256), pair_of(y, 1, 192, 256))

@@ -11,6 +11,7 @@ U8 = mybir.dt.uint8
 FP8X4 = mybir.dt.float8_e4m3fn_x4
 MULT = mybir.AluOpType.mult
 SUBTRACT = mybir.AluOpType.subtract
+COPY = mybir.ActivationFunctionType.Copy
 SIGMOID = mybir.ActivationFunctionType.Sigmoid
 
 P = 128
@@ -107,14 +108,16 @@ def tile_attend_plw_gatekey_f_topk_kernel(tc, qT, kT, gT, th, offs, offs2, out_0
         for first, last in zip(cuts, cuts[1:]):
             gate_keys(3, first, last)
         weave_u(nc.scalar.copy, 1, cuts[0], cuts[1])
-        weave_q(nc.scalar.copy, 0)
+        one = held.tile([P, 1], F32, name="one", tag="one", align_bytes=64)
+        nc.gpsimd.memset(one[:], 1.0)
+        weave_q(lambda out, in_: nc.scalar.activation(out, in_, COPY, scale=one[:]), 0)
         weave_q(nc.scalar.copy, 1)
         weave_u(nc.vector.tensor_copy, 1, cuts[1], cuts[2])
         weave_u_tiles(nc.vector.tensor_copy, 1, 0, cuts[2], cuts[3])
         weave_u_tiles(nc.vector.tensor_copy, 1, 1, cuts[2], cuts[3])
         quantize_q(0)
 
-        u_all = held.tile([P, SLOTS], I32, name="u_all", tag="q_bf0", align_bytes=64)
+        u_all = held.tile([P, SLOTS], I32, name="u_all", tag="one", align_bytes=64)
         u_codes = [u_all[:, r * P : (r + 1) * P] for r in range(PACK)]
         u_scales = [held.tile([P, P], U8, name="u_scales%d" % r, align_bytes=64) for r in range(PACK)]
         for r in range(PACK):

@@ -30,7 +30,7 @@ def tile_attend_plw_gatekey_f_topk_kernel(tc, qT, kT, gT, th, offs, offs2, out_0
 
         key_list = held.tile([P, SLOTS // 16], U16, name="key_list")
         gate_list = held.tile([P, SLOTS // 16], U16, name="gate_list")
-        th_cols = held.tile([P, 2], F32, name="th_cols")
+        th_cols = held.tile([P, 8], F32, name="th_cols")
         gates = [held.tile([P, 2, GATES], F32, name="gates%d" % j) for j in range(2)]
         keys = [held.tile([P, TOKENS], F32, name="keys%d" % t) for t in range(PACK)]
         q_raw = held.tile([P, PACK, NQ], F32, name="q_raw", align_bytes=64)
@@ -42,7 +42,7 @@ def tile_attend_plw_gatekey_f_topk_kernel(tc, qT, kT, gT, th, offs, offs2, out_0
         nc.sync.dma_start(gates[0][:], g_rows[:, 0:2, :])
         nc.sync.dma_start(gate_list[:], offs2)
         nc.sync.dma_start(key_list[:], offs)
-        nc.sync.dma_start(th_cols[:], th.rearrange("a b (p c) -> (a b p) c", c=2))
+        nc.sync.dma_start(th_cols[0:32, :], th.rearrange("a b (p c) -> (a b p) c", c=8))
         nc.sync.dma_start(gates[1][:], g_rows[:, 2:4, :])
         for t in range(PACK):
             nc.sync.dma_start(keys[t][:], k_rows[:, t, :])
@@ -54,11 +54,17 @@ def tile_attend_plw_gatekey_f_topk_kernel(tc, qT, kT, gT, th, offs, offs2, out_0
         warm = held.tile([P, 1], F32, name="warm")
         nc.scalar.activation(warm[:], ident[:, 0:1], SIGMOID)
 
-        th_psum = psum.tile([P, 2, P], F32, name="th_psum", tag="acc11")
-        for c in range(2):
-            nc.tensor.transpose(th_psum[:, c, :], th_cols[:, c : c + 1].to_broadcast([P, P]), ident[:])
+        nc.gpsimd.memset(th_cols[32:64, :], 0.0)
+        nc.gpsimd.memset(th_cols[64:128, :], 0.0)
         th_all = held.tile([P, NQ], F32, name="th_all")
-        nc.scalar.copy(th_all[:].rearrange("p (k c) -> p k c", c=2), th_psum[:].rearrange("p c k -> p k c"))
+        for b, tag in enumerate(("acc01", "acc11")):
+            th_psum = psum.tile([P, 4, P], F32, name="th_psum%d" % b, tag=tag)
+            for c in range(4):
+                nc.tensor.transpose(th_psum[:, c, :], th_cols[:, 4 * b + c : 4 * b + c + 1].to_broadcast([P, P]), ident[:])
+            nc.scalar.copy(
+                th_all[:].rearrange("p (k c) -> p k c", c=8)[:, :, 4 * b : 4 * b + 4],
+                th_psum[:, :, 0:32].rearrange("p c k -> p k c"),
+            )
 
         picked = [held.tile([P, SLOTS], F32, name="picked%d" % t) for t in range(PACK)]
         for t in range(PACK):

@@ -110,17 +110,18 @@ def tile_attend_plw_gatekey_f_topk_kernel(tc, qT, kT, gT, th, offs, offs2, out_0
         gate_keys(1, 0, SLOTS)
         weave_u(nc.scalar.copy, 0, 0, SLOTS)
         gate_keys(2, 0, SLOTS)
-        cuts = (0, 128, 384, SLOTS)
+        cuts = (0, 96, 192, 384, SLOTS)
         for first, last in zip(cuts, cuts[1:]):
             gate_keys(3, first, last)
         weave_u(nc.scalar.copy, 1, cuts[0], cuts[1])
+        weave_u(nc.scalar.copy, 1, cuts[1], cuts[2])
         one = held.tile([P, 1], F32, name="one", tag="one", align_bytes=64)
         nc.gpsimd.memset(one[:], 1.0)
         weave_q(lambda out, in_: nc.scalar.activation(out, in_, COPY, scale=one[:]), 0)
         weave_q(nc.scalar.copy, 1)
-        weave_u(nc.vector.tensor_copy, 1, cuts[1], cuts[2])
-        weave_u_tiles(nc.vector.tensor_copy, 1, 0, cuts[2], cuts[3])
-        weave_u_tiles(nc.vector.tensor_copy, 1, 1, cuts[2], cuts[3])
+        weave_u(nc.vector.tensor_copy, 1, cuts[2], cuts[3])
+        weave_u_tiles(nc.vector.tensor_copy, 1, 0, cuts[3], cuts[4])
+        weave_u_tiles(nc.vector.tensor_copy, 1, 1, cuts[3], cuts[4])
         quantize_q(0)
 
         u_all = held.tile([P, SLOTS], I32, name="u_all", tag="one", align_bytes=64)

@@ -31,28 +31,32 @@ def tile_attend_plw_gatekey_f_topk_kernel(tc, qT, kT, gT, th, offs, offs2, out_0
         key_list = held.tile([P, SLOTS // 16], U16, name="key_list")
         gate_list = held.tile([P, SLOTS // 16], U16, name="gate_list")
         th_cols = held.tile([P, 8], F32, name="th_cols")
-        gates = [held.tile([P, 2, GATES], F32, name="gates%d" % j) for j in range(2)]
-        keys = [held.tile([P, TOKENS], F32, name="keys%d" % t) for t in range(PACK)]
+        gates = held.tile([P, PACK, GATES], F32, name="gates")
+        keys01 = held.tile([P, 2 * TOKENS], F32, name="keys01")
+        keys2 = held.tile([P, TOKENS], F32, name="keys2")
+        keys3 = held.tile([P, TOKENS], F32, name="keys3")
         q_raw = held.tile([P, PACK, NQ], F32, name="q_raw", align_bytes=64)
 
         g_rows = gT.rearrange("(p t) c -> p t c", t=PACK)
         k_rows = kT.rearrange("(p t) c -> p t c", t=PACK)
         q_rows = qT.rearrange("b (p t) c -> (b p) t c", t=PACK)
 
-        nc.sync.dma_start(gates[0][:], g_rows[:, 0:2, :])
+        nc.sync.dma_start(gates[:], g_rows)
         nc.sync.dma_start(gate_list[:], offs2)
         nc.sync.dma_start(key_list[:], offs)
         nc.sync.dma_start(th_cols[0:32, :], th.rearrange("a b (p c) -> (a b p) c", c=8))
-        nc.sync.dma_start(gates[1][:], g_rows[:, 2:4, :])
-        for t in range(PACK):
-            nc.sync.dma_start(keys[t][:], k_rows[:, t, :])
+        nc.sync.dma_start(keys01[:].rearrange("p (t c) -> p t c", t=2), k_rows[:, 0:2, :])
+        nc.sync.dma_start(keys2[:], k_rows[:, 2, :])
+        nc.sync.dma_start(keys3[:], k_rows[:, 3, :])
         nc.sync.dma_start(q_raw[:], q_rows)
 
+        one = held.tile([P, 1], F32, name="one", tag="one", align_bytes=64)
+        nc.gpsimd.memset(one[:], 1.0)
         ident = held.tile([P, P], F32, name="ident")
         make_identity(nc, ident[:])
 
         warm = held.tile([P, 1], F32, name="warm")
-        nc.scalar.activation(warm[:], ident[:, 0:1], SIGMOID)
+        nc.scalar.activation(warm[:], one[:], SIGMOID)
 
         nc.gpsimd.memset(th_cols[32:64, :], 0.0)
         nc.gpsimd.memset(th_cols[64:128, :], 0.0)
@@ -67,18 +71,29 @@ def tile_attend_plw_gatekey_f_topk_kernel(tc, qT, kT, gT, th, offs, offs2, out_0
             )
 
         picked = [held.tile([P, SLOTS], F32, name="picked%d" % t) for t in range(PACK)]
-        for t in range(PACK):
-            nc.vector.tensor_copy(picked[t][:], gates[t // 2][:, t % 2, :].indirect(gate_list[:]))
+        for t in range(3):
+            nc.vector.tensor_copy(picked[t][:], gates[:, t, :].indirect(gate_list[:]))
+        for t in range(3, PACK):
+            nc.scalar.activation(picked[t][:], gates[:, t, :].indirect(gate_list[:]), COPY)
+        key_picked = [held.tile([P, SLOTS], F32, name="key_picked%d" % j) for j in range(2)]
 
         u_pair = [held.tile([P, 2, SLOTS], F32, name="u_pair%d" % j) for j in range(2)]
         u_bf = held.tile([P, PACK, P, PACK], BF16, name="u_bf", align_bytes=64)
 
-        def gate_keys(t, first, last):
+        def gate_keys(t, window, first, last):
             nc.vector.tensor_tensor(
                 u_pair[t // 2][:, t % 2, first:last],
-                keys[t][:].indirect(key_list[:, first // 16 : last // 16]),
+                window.indirect(key_list[:, first // 16 : last // 16]),
                 picked[t][:, first:last],
                 MULT,
+            )
+
+        def pick_keys(t, window, first, last):
+            nc.scalar.activation(key_picked[t // 2][:, first:last], window.indirect(key_list[:, first // 16 : last // 16]), COPY)
+
+        def gate_picked(t, first, last):
+            nc.vector.tensor_tensor(
+                u_pair[t // 2][:, t % 2, first:last], key_picked[t // 2][:, first:last], picked[t][:, first:last], MULT
             )
 
         def weave_u(copy, j, first, last):
@@ -106,22 +121,21 @@ def tile_attend_plw_gatekey_f_topk_kernel(tc, qT, kT, gT, th, offs, offs2, out_0
         def quantize_q(h):
             nc.vector.quantize_mx(q_codes[h][:].bitcast(FP8X4), q_scales[h][:], q_bf[h][:].rearrange("p c t -> p (c t)"))
 
-        gate_keys(0, 0, SLOTS)
-        gate_keys(1, 0, SLOTS)
+        gate_keys(0, keys01[:], 0, SLOTS)
+        pick_keys(1, keys01[:, TOKENS : 2 * TOKENS], 0, SLOTS)
+        gate_picked(1, 0, SLOTS)
         weave_u(nc.scalar.copy, 0, 0, SLOTS)
-        gate_keys(2, 0, SLOTS)
-        cuts = (0, 96, 192, 384, SLOTS)
-        for first, last in zip(cuts, cuts[1:]):
-            gate_keys(3, first, last)
-        weave_u(nc.scalar.copy, 1, cuts[0], cuts[1])
-        weave_u(nc.scalar.copy, 1, cuts[1], cuts[2])
-        one = held.tile([P, 1], F32, name="one", tag="one", align_bytes=64)
-        nc.gpsimd.memset(one[:], 1.0)
+        gate_keys(2, keys2[:], 0, SLOTS)
+        gate_keys(3, keys3[:], 0, 192)
+        pick_keys(3, keys3[:], 192, 352)
+        pick_keys(3, keys3[:], 352, SLOTS)
         weave_q(lambda out, in_: nc.scalar.activation(out, in_, COPY, scale=one[:]), 0)
         weave_q(nc.scalar.copy, 1)
-        weave_u(nc.vector.tensor_copy, 1, cuts[2], cuts[3])
-        weave_u_tiles(nc.vector.tensor_copy, 1, 0, cuts[3], cuts[4])
-        weave_u_tiles(nc.vector.tensor_copy, 1, 1, cuts[3], cuts[4])
+        gate_picked(3, 192, 352)
+        weave_u(nc.vector.tensor_copy, 1, 0, 192)
+        gate_picked(3, 352, SLOTS)
+        weave_u(nc.vector.tensor_copy, 1, 192, 352)
+        weave_u(nc.vector.tensor_copy, 1, 352, SLOTS)
         quantize_q(0)
 
         u_all = held.tile([P, SLOTS], I32, name="u_all", tag="one", align_bytes=64)

@@ -122,32 +122,42 @@ def tile_attend_plw_gatekey_f_topk_kernel(tc, qT, kT, gT, th, offs, offs2, out_0
             nc.vector.quantize_mx(q_codes[h][:].bitcast(FP8X4), q_scales[h][:], q_bf[h][:].rearrange("p c t -> p (c t)"))
 
         gate_keys(0, keys01[:], 0, SLOTS)
-        pick_keys(1, keys01[:, TOKENS : 2 * TOKENS], 0, SLOTS)
-        gate_picked(1, 0, SLOTS)
-        weave_u(nc.scalar.copy, 0, 0, SLOTS)
+        for first in (0, SLOTS // 2):
+            pick_keys(1, keys01[:, TOKENS : 2 * TOKENS], first, first + SLOTS // 2)
+            gate_picked(1, first, first + SLOTS // 2)
+        for first in (0, SLOTS // 2):
+            weave_u(nc.scalar.copy, 0, first, first + SLOTS // 2)
         gate_keys(2, keys2[:], 0, SLOTS)
-        gate_keys(3, keys3[:], 0, 192)
-        pick_keys(3, keys3[:], 192, 352)
+        gate_keys(3, keys3[:], 0, 224)
+        pick_keys(3, keys3[:], 224, 352)
         pick_keys(3, keys3[:], 352, SLOTS)
+        weave_u(nc.scalar.copy, 1, 0, 64)
         weave_q(lambda out, in_: nc.scalar.activation(out, in_, COPY, scale=one[:]), 0)
         weave_q(nc.scalar.copy, 1)
-        gate_picked(3, 192, 352)
-        weave_u(nc.vector.tensor_copy, 1, 0, 192)
+        gate_picked(3, 224, 352)
+        weave_u(nc.vector.tensor_copy, 1, 64, 224)
         gate_picked(3, 352, SLOTS)
-        weave_u(nc.vector.tensor_copy, 1, 192, 352)
+        weave_u(nc.vector.tensor_copy, 1, 224, 352)
         weave_u(nc.vector.tensor_copy, 1, 352, SLOTS)
         quantize_q(0)
 
         u_all = held.tile([P, SLOTS], I32, name="u_all", tag="one", align_bytes=64)
         u_codes = [u_all[:, r * P : (r + 1) * P] for r in range(PACK)]
         u_scales = [held.tile([P, P], U8, name="u_scales%d" % r, align_bytes=64) for r in range(PACK)]
-        for r in range(PACK):
+
+        def quantize_u(r):
             nc.vector.quantize_mx(u_codes[r].bitcast(FP8X4), u_scales[r][:], u_bf[:, r, :, :].rearrange("p s t -> p (s t)"))
+
+        for r in range(PACK):
+            quantize_u(r)
         quantize_q(1)
 
         z = held.tile([P, PACK, NQ], F32, name="z", align_bytes=64)
         y = held.tile([P, PACK, NQ], F32, name="y", align_bytes=64)
-        y_bf = held.tile([P, NQ, PACK], BF16, name="y_bf", align_bytes=64)
+        y_parts = {
+            (first, last): held.tile([P, last - first, PACK], BF16, name="y_bf%d" % first, align_bytes=64)
+            for first, last in ((0, 128), (128, 192), (192, NQ))
+        }
         y_codes = held.tile([P, NQ], I32, name="y_codes", align_bytes=64)
         y_scales = held.tile([P, NQ], U8, name="y_scales", align_bytes=64)
         out_rows = out_0.rearrange("(p r) q -> p r q", r=PACK)
@@ -180,7 +190,7 @@ def tile_attend_plw_gatekey_f_topk_kernel(tc, qT, kT, gT, th, offs, offs2, out_0
             sigmoid(r, h * QH, (h + 1) * QH)
 
         def woven(first, last):
-            return y_bf[:, first:last, :].rearrange("p (c i) r -> p c r i", i=4)
+            return y_parts[first, last][:].rearrange("p (c i) r -> p c r i", i=4)
 
         def by_tile(src, first, last):
             return src[:, :, first:last].rearrange("p r (c i) -> p c r i", i=4)
@@ -192,17 +202,11 @@ def tile_attend_plw_gatekey_f_topk_kernel(tc, qT, kT, gT, th, offs, offs2, out_0
             nc.vector.quantize_mx(
                 y_codes[:, first:last].bitcast(FP8X4),
                 y_scales[:, first:last],
-                y_bf[:, first:last, :].rearrange("p c r -> p (c r)"),
+                y_parts[first, last][:].rearrange("p c r -> p (c r)"),
             )
 
         def store_rows(first, last):
             nc.sync.dma_start(out_rows[:, first:last, :], y[:, first:last, :])
-
-        def woven_pair(j, first, last):
-            return y_bf[:, first:last, 2 * j : 2 * j + 2].rearrange("p (c i) r -> p c r i", i=4)
-
-        def pair_of(src, j, first, last):
-            return src[:, 2 * j : 2 * j + 2, first:last].rearrange("p r (c i) -> p c r i", i=4)
 
         score(0, 0)
         score(1, 0)
@@ -213,19 +217,18 @@ def tile_attend_plw_gatekey_f_topk_kernel(tc, qT, kT, gT, th, offs, offs2, out_0
         score(3, 1)
         store_rows(2, 4)
         multiply(0, 1)
-        subtract(0, 128, 256)
+        subtract(0, 128, NQ)
         multiply(1, 1)
         subtract(1, 128, 192)
-        subtract(1, 192, 256)
+        subtract(1, 192, NQ)
         nc.scalar.activation(y[:, 0:2, 128:192], z[:, 0:2, 128:192], SIGMOID)
-        nc.scalar.activation(woven_pair(0, 192, 256), pair_of(z, 0, 192, 256), SIGMOID)
-        nc.scalar.activation(y[:, 0:2, 192:256], z[:, 0:2, 192:256], SIGMOID)
+        nc.scalar.activation(woven(192, NQ), by_tile(z, 192, NQ), SIGMOID)
+        nc.scalar.activation(y[:, 0:2, 192:NQ], z[:, 0:2, 192:NQ], SIGMOID)
         nc.sync.dma_start(out_rows[:, 0:2, QH:NQ], y[:, 0:2, QH:NQ])
         weave_y(0, 128)
-        nc.vector.tensor_copy(woven_pair(1, 192, 256), pair_of(y, 1, 192, 256))
         weave_y(128, 192)
         quantize_y(0, 128)
-        quantize_y(192, 256)
+        quantize_y(192, NQ)
         quantize_y(128, 192)
         nc.sync.dma_start(words, y_codes[:])
         for quadrant in range(4):

@@ -222,10 +222,11 @@ def tile_attend_plw_gatekey_f_topk_kernel(tc, qT, kT, gT, th, offs, offs2, out_0
         subtract(1, 128, 192)
         subtract(1, 192, NQ)
         nc.scalar.activation(y[:, 0:2, 128:192], z[:, 0:2, 128:192], SIGMOID)
-        nc.scalar.activation(woven(192, NQ), by_tile(z, 192, NQ), SIGMOID)
+        nc.scalar.activation(woven(192, NQ)[:, :, 0:2, :], by_tile(z, 192, NQ)[:, :, 0:2, :], SIGMOID)
         nc.scalar.activation(y[:, 0:2, 192:NQ], z[:, 0:2, 192:NQ], SIGMOID)
         nc.sync.dma_start(out_rows[:, 0:2, QH:NQ], y[:, 0:2, QH:NQ])
         weave_y(0, 128)
+        nc.vector.tensor_copy(woven(192, NQ)[:, :, 2:4, :], by_tile(y, 192, NQ)[:, :, 2:4, :])
         weave_y(128, 192)
         quantize_y(0, 128)
         quantize_y(192, NQ)

@@ -35,7 +35,7 @@ def tile_attend_plw_gatekey_f_topk_kernel(tc, qT, kT, gT, th, offs, offs2, out_0
         keys01 = held.tile([P, 2 * TOKENS], F32, name="keys01")
         keys2 = held.tile([P, TOKENS], F32, name="keys2")
         keys3 = held.tile([P, TOKENS], F32, name="keys3")
-        q_raw = held.tile([P, PACK, NQ], F32, name="q_raw", align_bytes=64)
+        q_raw = held.tile([P, PACK, NQ], F32, name="q_raw", align_bytes=256)
 
         g_rows = gT.rearrange("(p t) c -> p t c", t=PACK)
         k_rows = kT.rearrange("(p t) c -> p t c", t=PACK)
@@ -50,7 +50,7 @@ def tile_attend_plw_gatekey_f_topk_kernel(tc, qT, kT, gT, th, offs, offs2, out_0
         nc.sync.dma_start(keys3[:], k_rows[:, 3, :])
         nc.sync.dma_start(q_raw[:], q_rows)
 
-        one = held.tile([P, 1], F32, name="one", tag="one", align_bytes=64)
+        one = held.tile([P, 1], F32, name="one", tag="one", align_bytes=256)
         nc.gpsimd.memset(one[:], 1.0)
         ident = held.tile([P, P], F32, name="ident")
         make_identity(nc, ident[:])
@@ -78,7 +78,7 @@ def tile_attend_plw_gatekey_f_topk_kernel(tc, qT, kT, gT, th, offs, offs2, out_0
         key_picked = [held.tile([P, SLOTS], F32, name="key_picked%d" % j) for j in range(2)]
 
         u_pair = [held.tile([P, 2, SLOTS], F32, name="u_pair%d" % j) for j in range(2)]
-        u_bf = held.tile([P, PACK, P, PACK], BF16, name="u_bf", align_bytes=64)
+        u_bf = held.tile([P, PACK, P, PACK], BF16, name="u_bf", align_bytes=256)
 
         def gate_keys(t, window, first, last):
             nc.vector.tensor_tensor(
@@ -108,9 +108,9 @@ def tile_attend_plw_gatekey_f_topk_kernel(tc, qT, kT, gT, th, offs, offs2, out_0
                 u_pair[j][:, :, first:last].rearrange("p t (s a b) -> p a s t b", a=2, b=2)[:, a],
             )
 
-        q_bf = [held.tile([P, QH, PACK], BF16, name="q_bf%d" % h, tag="q_bf%d" % h, align_bytes=64) for h in range(HALVES)]
-        q_codes = [held.tile([P, QH], I32, name="q_codes%d" % h, align_bytes=64) for h in range(HALVES)]
-        q_scales = [held.tile([P, QH], U8, name="q_scales%d" % h, align_bytes=64) for h in range(HALVES)]
+        q_bf = [held.tile([P, QH, PACK], BF16, name="q_bf%d" % h, tag="q_bf%d" % h, align_bytes=256) for h in range(HALVES)]
+        q_codes = [held.tile([P, QH], I32, name="q_codes%d" % h, align_bytes=256) for h in range(HALVES)]
+        q_scales = [held.tile([P, QH], U8, name="q_scales%d" % h, align_bytes=256) for h in range(HALVES)]
 
         def weave_q(copy, h):
             copy(
@@ -141,9 +141,9 @@ def tile_attend_plw_gatekey_f_topk_kernel(tc, qT, kT, gT, th, offs, offs2, out_0
         weave_u(nc.vector.tensor_copy, 1, 352, SLOTS)
         quantize_q(0)
 
-        u_all = held.tile([P, SLOTS], I32, name="u_all", tag="one", align_bytes=64)
+        u_all = held.tile([P, SLOTS], I32, name="u_all", tag="one", align_bytes=256)
         u_codes = [u_all[:, r * P : (r + 1) * P] for r in range(PACK)]
-        u_scales = [held.tile([P, P], U8, name="u_scales%d" % r, align_bytes=64) for r in range(PACK)]
+        u_scales = [held.tile([P, P], U8, name="u_scales%d" % r, align_bytes=256) for r in range(PACK)]
 
         def quantize_u(r):
             nc.vector.quantize_mx(u_codes[r].bitcast(FP8X4), u_scales[r][:], u_bf[:, r, :, :].rearrange("p s t -> p (s t)"))
@@ -152,14 +152,14 @@ def tile_attend_plw_gatekey_f_topk_kernel(tc, qT, kT, gT, th, offs, offs2, out_0
             quantize_u(r)
         quantize_q(1)
 
-        z = held.tile([P, PACK, NQ], F32, name="z", align_bytes=64)
-        y = held.tile([P, PACK, NQ], F32, name="y", align_bytes=64)
+        z = held.tile([P, PACK, NQ], F32, name="z", align_bytes=256)
+        y = held.tile([P, PACK, NQ], F32, name="y", align_bytes=256)
         y_parts = {
-            (first, last): held.tile([P, last - first, PACK], BF16, name="y_bf%d" % first, align_bytes=64)
+            (first, last): held.tile([P, last - first, PACK], BF16, name="y_bf%d" % first, align_bytes=256)
             for first, last in ((0, 128), (128, 192), (192, NQ))
         }
-        y_codes = held.tile([P, NQ], I32, name="y_codes", align_bytes=64)
-        y_scales = held.tile([P, NQ], U8, name="y_scales", align_bytes=64)
+        y_codes = held.tile([P, NQ], I32, name="y_codes", align_bytes=256)
+        y_scales = held.tile([P, NQ], U8, name="y_scales", align_bytes=256)
         out_rows = out_0.rearrange("(p r) q -> p r q", r=PACK)
         words = out_1.rearrange("s p q x -> (s p) (q x)").bitcast(I32)
         scale_rows = out_2.rearrange("s f q -> (s f) q").bitcast(I32)

from contextlib import ExitStack

import concourse.mybir as mybir
from concourse.masks import make_identity

F32 = mybir.dt.float32
BF16 = mybir.dt.bfloat16
I32 = mybir.dt.int32
U16 = mybir.dt.uint16
U8 = mybir.dt.uint8
FP8X4 = mybir.dt.float8_e4m3fn_x4
MULT = mybir.AluOpType.mult
SUBTRACT = mybir.AluOpType.subtract
COPY = mybir.ActivationFunctionType.Copy
SIGMOID = mybir.ActivationFunctionType.Sigmoid

P = 128
PACK = 4
SLOTS, TOKENS, GATES, D, NQ = 512, 2048, 1024, 512, 256
HALVES = 2
QH = NQ // HALVES
FLOPS = 2 * SLOTS * D * NQ


def tile_attend_plw_gatekey_f_topk_kernel(tc, qT, kT, gT, th, offs, offs2, out_0, out_1, out_2):
    nc = tc.nc
    with ExitStack() as ctx:
        held = ctx.enter_context(tc.tile_pool(name="held", bufs=1))
        psum = ctx.enter_context(tc.psum_pool(name="psum", bufs=1))

        key_list = held.tile([P, SLOTS // 16], U16, name="key_list")
        gate_list = held.tile([P, SLOTS // 16], U16, name="gate_list")
        th_cols = held.tile([P, 8], F32, name="th_cols")
        gates = held.tile([P, PACK, GATES], F32, name="gates")
        keys01 = held.tile([P, 2 * TOKENS], F32, name="keys01")
        keys2 = held.tile([P, TOKENS], F32, name="keys2")
        keys3 = held.tile([P, TOKENS], F32, name="keys3")
        q_raw = held.tile([P, PACK, NQ], F32, name="q_raw", align_bytes=256)

        g_rows = gT.rearrange("(p t) c -> p t c", t=PACK)
        k_rows = kT.rearrange("(p t) c -> p t c", t=PACK)
        q_rows = qT.rearrange("b (p t) c -> (b p) t c", t=PACK)

        nc.sync.dma_start(gates[:], g_rows)
        nc.sync.dma_start(gate_list[:], offs2)
        nc.sync.dma_start(key_list[:], offs)
        nc.sync.dma_start(th_cols[0:32, :], th.rearrange("a b (p c) -> (a b p) c", c=8))
        nc.sync.dma_start(keys01[:].rearrange("p (t c) -> p t c", t=2), k_rows[:, 0:2, :])
        nc.sync.dma_start(keys2[:], k_rows[:, 2, :])
        nc.sync.dma_start(keys3[:], k_rows[:, 3, :])
        nc.sync.dma_start(q_raw[:], q_rows)

        one = held.tile([P, 1], F32, name="one", tag="one", align_bytes=256)
        nc.gpsimd.memset(one[:], 1.0)
        ident = held.tile([P, P], F32, name="ident")
        make_identity(nc, ident[:])

        warm = held.tile([P, 1], F32, name="warm")
        nc.scalar.activation(warm[:], one[:], SIGMOID)

        nc.gpsimd.memset(th_cols[32:64, :], 0.0)
        nc.gpsimd.memset(th_cols[64:128, :], 0.0)
        th_all = held.tile([P, NQ], F32, name="th_all")
        for b, tag in enumerate(("acc01", "acc11")):
            th_psum = psum.tile([P, 4, P], F32, name="th_psum%d" % b, tag=tag)
            for c in range(4):
                nc.tensor.transpose(th_psum[:, c, :], th_cols[:, 4 * b + c : 4 * b + c + 1].to_broadcast([P, P]), ident[:])
            nc.scalar.copy(
                th_all[:].rearrange("p (k c) -> p k c", c=8)[:, :, 4 * b : 4 * b + 4],
                th_psum[:, :, 0:32].rearrange("p c k -> p k c"),
            )

        picked = [held.tile([P, SLOTS], F32, name="picked%d" % t) for t in range(PACK)]
        for t in range(3):
            nc.vector.tensor_copy(picked[t][:], gates[:, t, :].indirect(gate_list[:]))
        for t in range(3, PACK):
            nc.scalar.activation(picked[t][:], gates[:, t, :].indirect(gate_list[:]), COPY)
        key_picked = [held.tile([P, SLOTS], F32, name="key_picked%d" % j) for j in range(2)]

        u_pair = [held.tile([P, 2, SLOTS], F32, name="u_pair%d" % j) for j in range(2)]
        u_bf = held.tile([P, PACK, P, PACK], BF16, name="u_bf", align_bytes=256)

        def gate_keys(t, window, first, last):
            nc.vector.tensor_tensor(
                u_pair[t // 2][:, t % 2, first:last],
                window.indirect(key_list[:, first // 16 : last // 16]),
                picked[t][:, first:last],
                MULT,
            )

        def pick_keys(t, window, first, last):
            nc.scalar.activation(key_picked[t // 2][:, first:last], window.indirect(key_list[:, first // 16 : last // 16]), COPY)

        def gate_picked(t, first, last):
            nc.vector.tensor_tensor(
                u_pair[t // 2][:, t % 2, first:last], key_picked[t // 2][:, first:last], picked[t][:, first:last], MULT
            )

        def weave_u(copy, j, first, last):
            copy(
                u_bf[:, :, first // PACK : last // PACK, 2 * j : 2 * j + 2].rearrange("p (a b) s t -> p a s t b", b=2),
                u_pair[j][:, :, first:last].rearrange("p t (s a b) -> p a s t b", a=2, b=2),
            )

        def weave_u_tiles(copy, j, a, first, last):
            copy(
                u_bf[:, 2 * a : 2 * a + 2, first // PACK : last // PACK, 2 * j : 2 * j + 2].rearrange("p b s t -> p s t b"),
                u_pair[j][:, :, first:last].rearrange("p t (s a b) -> p a s t b", a=2, b=2)[:, a],
            )

        q_bf = [held.tile([P, QH, PACK], BF16, name="q_bf%d" % h, tag="q_bf%d" % h, align_bytes=256) for h in range(HALVES)]
        q_codes = [held.tile([P, QH], I32, name="q_codes%d" % h, align_bytes=256) for h in range(HALVES)]
        q_scales = [held.tile([P, QH], U8, name="q_scales%d" % h, align_bytes=256) for h in range(HALVES)]

        def weave_q(copy, h):
            copy(
                q_bf[h][:].rearrange("p (c i) t -> p c t i", i=4),
                q_raw[:, :, h * QH : (h + 1) * QH].rearrange("p t (c i) -> p c t i", i=4),
            )

        def quantize_q(h):
            nc.vector.quantize_mx(q_codes[h][:].bitcast(FP8X4), q_scales[h][:], q_bf[h][:].rearrange("p c t -> p (c t)"))

        gate_keys(0, keys01[:], 0, SLOTS)
        for first in (0, SLOTS // 2):
            pick_keys(1, keys01[:, TOKENS : 2 * TOKENS], first, first + SLOTS // 2)
            gate_picked(1, first, first + SLOTS // 2)
        for first in (0, SLOTS // 2):
            weave_u(nc.scalar.copy, 0, first, first + SLOTS // 2)
        gate_keys(2, keys2[:], 0, SLOTS)
        gate_keys(3, keys3[:], 0, 224)
        pick_keys(3, keys3[:], 224, 352)
        pick_keys(3, keys3[:], 352, SLOTS)
        weave_u(nc.scalar.copy, 1, 0, 64)
        weave_q(lambda out, in_: nc.scalar.activation(out, in_, COPY, scale=one[:]), 0)
        weave_q(nc.scalar.copy, 1)
        gate_picked(3, 224, 352)
        weave_u(nc.vector.tensor_copy, 1, 64, 224)
        gate_picked(3, 352, SLOTS)
        weave_u(nc.vector.tensor_copy, 1, 224, 352)
        weave_u(nc.vector.tensor_copy, 1, 352, SLOTS)
        quantize_q(0)

        u_all = held.tile([P, SLOTS], I32, name="u_all", tag="one", align_bytes=256)
        u_codes = [u_all[:, r * P : (r + 1) * P] for r in range(PACK)]
        u_scales = [held.tile([P, P], U8, name="u_scales%d" % r, align_bytes=256) for r in range(PACK)]

        def quantize_u(r):
            nc.vector.quantize_mx(u_codes[r].bitcast(FP8X4), u_scales[r][:], u_bf[:, r, :, :].rearrange("p s t -> p (s t)"))

        for r in range(PACK):
            quantize_u(r)
        quantize_q(1)

        z = held.tile([P, PACK, NQ], F32, name="z", align_bytes=256)
        y = held.tile([P, PACK, NQ], F32, name="y", align_bytes=256)
        y_parts = {
            (first, last): held.tile([P, last - first, PACK], BF16, name="y_bf%d" % first, align_bytes=256)
            for first, last in ((0, 128), (128, 192), (192, NQ))
        }
        y_codes = held.tile([P, NQ], I32, name="y_codes", align_bytes=256)
        y_scales = held.tile([P, NQ], U8, name="y_scales", align_bytes=256)
        out_rows = out_0.rearrange("(p r) q -> p r q", r=PACK)
        words = out_1.rearrange("s p q x -> (s p) (q x)").bitcast(I32)
        scale_rows = out_2.rearrange("s f q -> (s f) q").bitcast(I32)
        acc = {}

        def multiply(r, h):
            acc[r, h] = psum.tile([P, QH], F32, name="acc%d%d" % (h, r), tag="acc%d%d" % (h, r))
            nc.tensor.matmul_mx(
                acc[r, h][:],
                lhsT=u_codes[r].bitcast(FP8X4),
                lhsT_scale=u_scales[r][:],
                rhs=q_codes[h][:].bitcast(FP8X4),
                rhs_scale=q_scales[h][:],
                start=True,
                stop=True,
            )

        def subtract(r, first, last):
            h = first // QH
            nc.vector.tensor_tensor(z[:, r, first:last], acc[r, h][:, first - h * QH : last - h * QH], th_all[:, first:last], SUBTRACT)

        def sigmoid(r, first, last):
            nc.scalar.activation(y[:, r, first:last], z[:, r, first:last], SIGMOID)

        def score(r, h):
            multiply(r, h)
            subtract(r, h * QH, (h + 1) * QH)
            sigmoid(r, h * QH, (h + 1) * QH)

        def woven(first, last):
            return y_parts[first, last][:].rearrange("p (c i) r -> p c r i", i=4)

        def by_tile(src, first, last):
            return src[:, :, first:last].rearrange("p r (c i) -> p c r i", i=4)

        def weave_y(first, last):
            nc.vector.tensor_copy(woven(first, last), by_tile(y, first, last))

        def quantize_y(first, last):
            nc.vector.quantize_mx(
                y_codes[:, first:last].bitcast(FP8X4),
                y_scales[:, first:last],
                y_parts[first, last][:].rearrange("p c r -> p (c r)"),
            )

        def store_rows(first, last):
            nc.sync.dma_start(out_rows[:, first:last, :], y[:, first:last, :])

        score(0, 0)
        score(1, 0)
        nc.sync.dma_start(out_rows[:, 0:2, 0:QH], y[:, 0:2, 0:QH])
        score(2, 0)
        score(3, 0)
        score(2, 1)
        score(3, 1)
        store_rows(2, 4)
        multiply(0, 1)
        subtract(0, 128, NQ)
        multiply(1, 1)
        subtract(1, 128, 192)
        subtract(1, 192, NQ)
        nc.scalar.activation(y[:, 0:2, 128:192], z[:, 0:2, 128:192], SIGMOID)
        nc.scalar.activation(woven(192, NQ)[:, :, 0:2, :], by_tile(z, 192, NQ)[:, :, 0:2, :], SIGMOID)
        nc.scalar.activation(y[:, 0:2, 192:NQ], z[:, 0:2, 192:NQ], SIGMOID)
        nc.sync.dma_start(out_rows[:, 0:2, QH:NQ], y[:, 0:2, QH:NQ])
        weave_y(0, 128)
        nc.vector.tensor_copy(woven(192, NQ)[:, :, 2:4, :], by_tile(y, 192, NQ)[:, :, 2:4, :])
        weave_y(128, 192)
        quantize_y(0, 128)
        quantize_y(192, NQ)
        quantize_y(128, 192)
        nc.sync.dma_start(words, y_codes[:])
        for quadrant in range(4):
            queue = nc.scalar if quadrant % 2 == 0 else nc.sync
            queue.dma_start(
                scale_rows[4 * quadrant : 4 * quadrant + 4, :],
                y_scales[32 * quadrant : 32 * quadrant + 4, :].bitcast(I32),
            )
